import numpy as np
import ml_dtypes


def mxq(x, axis, fmt="e4m3"):
    dtype, down = {"e4m3": (ml_dtypes.float8_e4m3fn, 7), "e5m2": (ml_dtypes.float8_e5m2, 14)}[fmt]
    v = np.moveaxis(np.asarray(x, np.float32).astype(ml_dtypes.bfloat16).astype(np.float64), axis, -1)
    blocks = v.reshape(v.shape[:-1] + (-1, 32))
    amax = np.abs(blocks).max(-1, keepdims=True)
    byte = np.maximum(np.where(amax > 0, np.frexp(amax)[1] - 1 + 127, 0) - down, 1)
    scale = np.exp2(byte - 127.0)
    codes = (blocks / scale).astype(np.float32).astype(dtype).astype(np.float64)
    return np.moveaxis((codes * scale).reshape(v.shape), -1, axis)


WIDE = False


def mx_kscale(k):
    if not WIDE:
        return np.ones(k)
    levels = np.array([10, -10, 5, -5, 0])
    if k % 512:
        return np.exp2(np.random.permutation(np.resize(levels, k // 32))).repeat(32)
    a = np.empty((k // 512, 16))
    for p in range(k // 512):
        a[p, :8] = np.random.permutation(np.resize(levels, 8))
        for g in range(8):
            far = levels[np.abs(levels - a[p, g]) >= 10]
            a[p, g + 8] = far[np.random.randint(len(far))]
    return np.exp2(a.ravel()).repeat(32)


def f64(x):
    return np.asarray(x).astype(np.float64)


def striped(idx):
    return np.tile(idx.reshape(-1, 16).T, (8, 1)).astype(np.uint16)


def unstriped(offs):
    return offs[:16].T.reshape(-1).astype(np.int64)


def striped8(idx):
    return np.concatenate([x.reshape(-1, 16).T for x in idx]).astype(np.uint16)


def runs(offs, k):
    lists = np.stack([offs[16 * r : 16 * r + 16].T.reshape(-1) for r in range(8)]).astype(np.int64)
    return lists[np.arange(k) % 512 // 64]


def pack_weight(w):
    k, n = w.shape
    w = f64(np.asarray(w, np.float32).astype(ml_dtypes.bfloat16)).reshape(k // 32, 32, n)
    amax = np.abs(w).max(1)
    byte = np.clip(np.where(amax > 0, np.frexp(amax)[1] - 1 + 127 - 7, 1), 1, 254)
    scaled = (w * np.exp2(127.0 - byte)[:, None, :]).reshape(k, n).astype(np.float32)
    words = np.ascontiguousarray(scaled.reshape(k // 512, 128, 4, n).transpose(0, 1, 3, 2)).astype(ml_dtypes.float8_e4m3fn).view(np.uint8)
    return words, np.ascontiguousarray(byte.astype(np.uint8).reshape(k // 512, 16, n))


def unpack_weight(words, scales):
    g, p, n, _ = words.shape
    vals = np.ascontiguousarray(words).view(ml_dtypes.float8_e4m3fn).astype(np.float64) * np.repeat(np.exp2(scales.astype(np.float64) - 127.0), 8, axis=1)[..., None]
    return vals.transpose(0, 1, 3, 2).reshape(g * 512, n)


E2M1 = np.array([0.0, 0.5, 1.0, 1.5, 2.0, 3.0, 4.0, 6.0, -0.0, -0.5, -1.0, -1.5, -2.0, -3.0, -4.0, -6.0])


def pack_fp4(w):
    k, n = w.shape
    w = f64(np.asarray(w, np.float32).astype(ml_dtypes.bfloat16)).reshape(k // 32, 32, n)
    amax = np.abs(w).max(1)
    mant, ex = np.frexp(amax / 6.0)
    byte = np.clip(np.where(amax > 0, np.where(mant > 0.5, ex, ex - 1) + 127, 1), 1, 254)
    scaled = (w * np.exp2(127.0 - byte)[:, None, :]).reshape(k, n).astype(np.float32)
    c = np.ascontiguousarray(scaled.reshape(k // 512, 128, 4, n).transpose(0, 1, 3, 2)).astype(ml_dtypes.float4_e2m1fn).view(np.uint8) & 0xF
    words = (c[..., 0::2] | (c[..., 1::2] << 4)).reshape(k // 512, 128, 2 * n)
    return np.ascontiguousarray(words), np.ascontiguousarray(byte.astype(np.uint8).reshape(k // 512, 16, n))


def unpack_fp4(words, scales):
    g, _, n = scales.shape
    words = np.ascontiguousarray(words).reshape(g, 128, n, 2)
    nib = np.empty((g, 128, n, 4), np.uint8)
    nib[..., 0::2] = words & 0xF
    nib[..., 1::2] = words >> 4
    vals = E2M1[nib] * np.repeat(np.exp2(scales.astype(np.float64) - 127.0), 8, axis=1)[..., None]
    return vals.transpose(0, 1, 3, 2).reshape(g * 512, n)


def sigmoid(v):
    return 1.0 / (1.0 + np.exp(-np.maximum(v, -700.0)))

def planes(y):
    n, m = y.shape
    v = y.astype(np.float32).astype(ml_dtypes.bfloat16).astype(np.float64).reshape(n // 32, 32, m)
    top = np.abs(v).max(1)
    byte = np.clip(np.where(top > 0, np.frexp(top)[1] - 1 + 127 - 7, 1), 1, 254)
    codes = (v * np.exp2(127.0 - byte)[:, None, :]).reshape(n, m).astype(np.float32).astype(ml_dtypes.float8_e4m3fn).view(np.uint8)
    words = codes.reshape(n // 512, 128, 4, m).transpose(0, 1, 3, 2)
    return np.ascontiguousarray(words), np.ascontiguousarray(byte.astype(np.uint8).reshape(n // 512, 16, m))


K, T, S, V, H, W = 512, 2048, 512, 512, 512, 256


def setup_inputs():
    n = np.random.standard_normal
    s = mx_kscale(K)[:, None]
    u = mx_kscale(S)
    packed_xT = pack_weight(n((K, T)) * s)
    packed_w1 = pack_fp4(n((K, H)) / np.sqrt(K) / s)
    packed_w2 = pack_fp4(n((K, H)) / np.sqrt(K) / s)
    perm = np.stack([np.random.permutation(S) for _ in range(8)])
    perm2 = np.stack([np.random.permutation(V) for _ in range(8)])
    return {
        "x_words": packed_xT[0],
        "x_scales": packed_xT[1],
        "w1_words": packed_w1[0],
        "w1_scales": packed_w1[1],
        "w2_words": packed_w2[0],
        "w2_scales": packed_w2[1],
        "ga": (np.random.uniform(0.5, 1.5, (H, 1)) * u[:, None]).astype(np.float32),
        "gb": (np.random.uniform(0.5, 1.5, (H, 1)) / u[:, None]).astype(np.float32),
        "offs": striped(np.random.permutation(T)[:S]),
        "two": striped(np.random.permutation(T)[:V]),
        "n1": striped8(perm[:, :W]),
        "n2": striped8(perm[:, W:]),
        "n3": striped8(np.stack([np.random.permutation(V) for _ in range(8)])),
        "n4": striped8(np.stack([np.random.permutation(V) for _ in range(8)])),
        "n5": striped8(perm2[:, :W]),
        "n6": striped8(perm2[:, W:]),
    }


def reference(x_words, x_scales, w1_words, w1_scales, w2_words, w2_scales, ga, gb, offs, two, n1, n2, n3, n4, n5, n6):
    xq = unpack_weight(x_words, x_scales)[:, unstriped(offs)]
    a = unpack_fp4(w1_words, w1_scales).T @ xq
    pa = a[np.arange(H)[:, None], runs(n1, H)]
    pb = a[np.arange(H)[:, None], runs(n2, H)]
    rb = pa * pb
    ra = pa + pb
    ds = np.zeros((H, S))
    ds[np.arange(H)[:, None], runs(n1, H)] = ra
    dt = ds.copy()
    dt[np.arange(H)[:, None], runs(n2, H)] = rb
    z = f64(ga) * dt
    x_two = unpack_weight(x_words, x_scales)[:, unstriped(two)]
    b = unpack_fp4(w2_words, w2_scales).T @ x_two
    sm = np.maximum(b, b[np.arange(H)[:, None], runs(n4, H)])
    ds2 = np.zeros((H, V))
    ds2[np.arange(H)[:, None], runs(n3, H)] = sm
    z2 = f64(gb) * (ds2 * sigmoid(b))
    s = 0.0625 * ((mxq(z, 0, "e4m3").T @ mxq(z2, 0, "e4m3")))
    pa2 = s[np.arange(S)[:, None], runs(n5, S)]
    pb2 = s[np.arange(S)[:, None], runs(n6, S)]
    rb2 = np.maximum(pa2, pb2)
    ra2 = pa2 / (np.abs(pb2) + 0.5)
    ds3 = np.zeros((S, V))
    ds3[np.arange(S)[:, None], runs(n5, S)] = ra2
    out = ds3.copy()
    out[np.arange(S)[:, None], runs(n6, S)] = rb2
    return (out,) + planes(out)

@@ -1,0 +1,295 @@
+from contextlib import ExitStack
+
+import concourse.mybir as mybir
+
+K, T, S, V, H, W = 512, 2048, 512, 512, 512, 256
+FLOPS = 3 * 2 * 512 * 512 * 512
+
+F32 = mybir.dt.float32
+BF16 = mybir.dt.bfloat16
+I32 = mybir.dt.int32
+U32 = mybir.dt.uint32
+U16 = mybir.dt.uint16
+U8 = mybir.dt.uint8
+FP8X4 = mybir.dt.float8_e4m3fn_x4
+FP4X4 = mybir.dt.float4_e2m1fn_x4
+ALU = mybir.AluOpType
+ACT = mybir.ActivationFunctionType
+
+P = 128
+PACK = 4
+
+
+def tile_picked_kqbondsendgratio_none_po_kernel(
+    tc, x_words, x_scales, w1_words, w1_scales, w2_words, w2_scales, ga, gb, offs, two, n1, n2, n3, n4, n5, n6, out_0, out_1, out_2
+):
+    nc = tc.nc
+    with ExitStack() as ctx:
+        keep = ctx.enter_context(tc.tile_pool(name="keep", bufs=1))
+        psum = ctx.enter_context(tc.psum_pool(name="psum", bufs=1))
+
+        def sb(name, shape, dtype, tag=None):
+            return keep.tile(shape, dtype, name=name, tag=tag or name, align_bytes=64)
+
+        def load_list(name, src):
+            t = keep.tile(list(src.shape), U16, name=name)
+            nc.sync.dma_start(t[:], src)
+            return t
+
+        def load_scales(name, src, width):
+            t = sb(name, [P, width], U8)
+            nc.vector.memset(t[:].bitcast(I32), 0)
+            rows = src[0].bitcast(I32)
+            for q in range(4):
+                nc.sync.dma_start(out=t[:].bitcast(I32)[32 * q : 32 * q + 4, :], in_=rows[4 * q : 4 * q + 4, :])
+            return t
+
+        def load_gain(name, src):
+            t = sb(name, [P, PACK], F32)
+            view = src.rearrange("(q t i) o -> i q (t o)", t=PACK, i=4)
+            with nc.allow_non_contiguous_dma(reason="one value a row"):
+                for i in range(4):
+                    nc.sync.dma_start(out=t[i:P:4, :], in_=view[i])
+            return t
+
+        def load_w(name, words, scales):
+            raw = sb(name + "_raw", [P, 2 * H], U8)
+            nc.sync.dma_start(out=raw[:].bitcast(I32), in_=words[0].bitcast(I32))
+            raw_s = load_scales(name + "_raw_s", scales, H)
+            return raw, raw_s
+
+        def deal_w(name, raw, raw_s, tags=(None, None)):
+            codes = sb(name + "_c", [P, 2 * H], U8, tags[0])
+            sc = sb(name + "_s", [P, H], U8, tags[1])
+            nc.vector.tensor_copy(
+                out=codes[:].bitcast(I32).rearrange("p (t q e) -> p t q e", t=PACK, e=2),
+                in_=raw[:].bitcast(I32).rearrange("p (q t e) -> p t q e", t=PACK, e=2),
+            )
+            nc.vector.tensor_copy(
+                out=sc[:].bitcast(I32).rearrange("p (t q) -> p t q", t=PACK),
+                in_=raw_s[:].bitcast(I32).rearrange("p (q t) -> p t q", t=PACK),
+            )
+            return codes, sc
+
+        w2_raw = sb("w2_raw", [P, 2 * H], U8)
+        nc.sync.dma_start(out=w2_raw[:].bitcast(I32), in_=w2_words[0].bitcast(I32))
+        xs = load_scales("xs", x_scales, T)
+        two_l = load_list("two_l", two)
+        xw = sb("xw", [P, T], I32)
+        nc.sync.dma_start(out=xw[:], in_=x_words[0].rearrange("p n r -> p (n r)").bitcast(I32))
+        offs_l = load_list("offs_l", offs)
+        w2_raw_s = load_scales("w2_raw_s", w2_scales, H)
+        n4_l = load_list("n4_l", n4)
+        n3_l = load_list("n3_l", n3)
+        w1_raw, w1_raw_s = load_w("w1", w1_words, w1_scales)
+        n1_l = load_list("n1_l", n1)
+        n2_l = load_list("n2_l", n2)
+        gb_t = load_gain("gb_t", gb)
+        ga_t = load_gain("ga_t", ga)
+        n5_l = load_list("n5_l", n5)
+        n6_l = load_list("n6_l", n6)
+
+        xb_s = sb("xb_s", [P, V], U8)
+        xa_s = sb("xa_s", [P, S], U8)
+        xb_w = sb("xb_w", [P, V], U32)
+        xa_w = sb("xa_w", [P, S], U32)
+        nc.vector.tensor_copy(xb_s[:], xs[:].indirect(two_l[:]))
+        nc.vector.tensor_copy(xa_s[:], xs[:].indirect(offs_l[:]))
+        w2_c, w2_s = deal_w("w2", w2_raw, w2_raw_s)
+        nc.vector.tensor_copy(xb_w[:], xw[:].bitcast(U32).indirect(two_l[:]))
+        nc.vector.tensor_copy(xa_w[:], xw[:].bitcast(U32).indirect(offs_l[:]))
+
+        def project(tag, codes, sc, xg_w, xg_s, t):
+            bank = psum.tile([P, 512], F32, name=f"{tag}{t}", tag=f"{tag}{t}")
+            nc.tensor.matmul_mx(
+                out=bank[:],
+                lhsT=codes[:, 256 * t : 256 * (t + 1)].bitcast(FP4X4),
+                lhsT_scale=sc[:, 128 * t : 128 * (t + 1)],
+                rhs=xg_w[:].bitcast(FP8X4),
+                rhs_scale=xg_s[:],
+                start=True,
+                stop=True,
+            )
+            return bank
+
+        b_bank = [project("bankb", w2_c, w2_s, xb_w, xb_s, t) for t in range(PACK)]
+        b_t = [sb(f"b{t}", [P, 2 * V], F32) for t in range(PACK)]
+        for t in range(PACK):
+            nc.scalar.copy(b_t[t][:, :V], b_bank[t][:])
+        sig = [sb(f"sig{t}", [P, V], F32) for t in range(PACK)]
+        for t in range(PACK):
+            nc.scalar.activation(sig[t][:], b_bank[t][:], ACT.Sigmoid)
+
+        bg = [sb(f"bg{t}", [P, V], F32) for t in range(PACK)]
+        sm = [sb(f"sm{t}", [P, V], F32) for t in range(PACK)]
+        ds2 = [sb(f"ds2_{t}", [P, 2 * V], F32) for t in range(PACK)]
+        z2_rows = sb("z2_rows", [P, PACK, V], BF16)
+
+        def b_gather(t):
+            nc.vector.tensor_copy(bg[t][:], b_t[t][:].indirect(n4_l[:]))
+
+        def b_max(t):
+            nc.vector.tensor_tensor(sm[t][:], bg[t][:], b_t[t][:, :V], ALU.max)
+
+        def b_scatter(t):
+            nc.vector.tensor_copy(ds2[t][:].indirect(n3_l[:]), sm[t][:])
+
+        def b_gate(t):
+            nc.vector.scalar_tensor_tensor(z2_rows[:, t, :], ds2[t][:, :V], gb_t[:, t : t + 1], sig[t][:], ALU.mult, ALU.mult)
+
+        pa = [sb(f"pa{t}", [P, W], F32) for t in range(PACK)]
+        pb = [sb(f"pb{t}", [P, W], F32) for t in range(PACK)]
+        dt = [sb(f"dt{t}", [P, S], F32) for t in range(PACK)]
+
+        def a_gather(t):
+            nc.vector.tensor_copy(pa[t][:], a_t[t][:].indirect(n1_l[:]))
+            nc.vector.tensor_copy(pb[t][:], a_t[t][:].indirect(n2_l[:]))
+
+        def a_sum(t):
+            nc.vector.tensor_tensor(dt[t][:].indirect(n1_l[:]), pa[t][:], pb[t][:], ALU.add)
+
+        def a_prod(t):
+            nc.vector.tensor_tensor(dt[t][:].indirect(n2_l[:]), pa[t][:], pb[t][:], ALU.mult)
+
+        b_gather(0)
+        b_gather(1)
+        b_max(0)
+        b_gather(2)
+        b_max(1)
+        b_scatter(0)
+        w1_c, w1_s = deal_w("w1", w1_raw, w1_raw_s, ("bg0", "bg1"))
+        a_bank = [project("banka", w1_c, w1_s, xa_w, xa_s, t) for t in range(PACK)]
+        a_t = [sb(f"a{t}", [P, S], F32) for t in range(PACK)]
+        for t in range(PACK):
+            nc.scalar.copy(a_t[t][:], a_bank[t][:])
+        b_gather(3)
+        b_max(2)
+        b_scatter(1)
+        b_max(3)
+        b_scatter(2)
+        b_gate(0)
+        b_scatter(3)
+        b_gate(1)
+        b_gate(2)
+        a_gather(0)
+        b_gate(3)
+
+        z2_g = sb("z2_g", [P, V, PACK], BF16)
+        nc.scalar.copy(
+            z2_g[:].rearrange("p (c i) t -> p c t i", i=4),
+            z2_rows[:].rearrange("p t (c i) -> p c t i", i=4),
+        )
+        z_g = sb("z_g", [P, PACK, 128, PACK], BF16)
+
+        def z_round(t, chunks):
+            if chunks:
+                for u in range(PACK):
+                    nc.scalar.activation(
+                        z_g[:, u, :, t], dt[t][:].rearrange("p (m u) -> p u m", u=PACK)[:, u, :], ACT.Copy, scale=ga_t[:, t : t + 1]
+                    )
+            else:
+                nc.scalar.activation(
+                    z_g[:, :, :, t].rearrange("p u m -> p m u"),
+                    dt[t][:].rearrange("p (m u) -> p m u", u=PACK),
+                    ACT.Copy,
+                    scale=ga_t[:, t : t + 1],
+                )
+
+        z2_c = sb("z2_c", [P, V], U32)
+        z2_s = sb("z2_s", [P, V], U8)
+        a_gather(1)
+        a_sum(0)
+        a_sum(1)
+        a_prod(0)
+        z_round(0, False)
+        a_gather(2)
+        a_prod(1)
+        z_round(1, False)
+        nc.vector.quantize_mx(out=z2_c[:].bitcast(FP8X4), scales=z2_s[:], in_=z2_g[:].rearrange("p c t -> p (c t)"))
+        a_sum(2)
+        a_gather(3)
+        a_prod(2)
+        z_round(2, False)
+        a_sum(3)
+        a_prod(3)
+        z_round(3, True)
+
+        s_t = [sb(f"s{u}", [P, V], F32) for u in range(PACK)]
+        for u in range(PACK):
+            z_c = sb(f"z_c{u}", [P, 128], U32)
+            z_s = sb(f"z_s{u}", [P, 128], U8)
+            nc.vector.quantize_mx(out=z_c[:].bitcast(FP8X4), scales=z_s[:], in_=z_g[:, u, :, :].rearrange("p m t -> p (m t)"))
+            bank = psum.tile([P, 512], F32, name=f"s_bank{u}", tag=f"bankb{u}")
+            nc.tensor.matmul_mx(
+                out=bank[:],
+                lhsT=z_c[:].bitcast(FP8X4),
+                lhsT_scale=z_s[:],
+                rhs=z2_c[:].bitcast(FP8X4),
+                rhs_scale=z2_s[:],
+                start=True,
+                stop=True,
+            )
+            nc.scalar.activation(s_t[u][:], bank[:], ACT.Copy, scale=0.0625)
+
+        pa2 = [sb(f"pa2_{u}", [P, W], F32) for u in range(PACK)]
+        pb2 = sb("pb2", [P, PACK, W], F32)
+        rb2 = [sb(f"rb2_{u}", [P, W], F32) for u in range(PACK)]
+        y = [sb(f"y{u}", [P, V], F32) for u in range(PACK)]
+        mag = sb("mag", [P, PACK * W], F32)
+        lg = sb("lg", [P, PACK * W], F32)
+        inv = sb("inv", [P, PACK, W], F32)
+        half = sb("half", [P, 1], F32)
+        nc.vector.memset(half[:], 0.5)
+        y_g = sb("y_g", [P, V, PACK], BF16)
+        out_rows = out_0.rearrange("(p u) v -> p u v", u=PACK)
+
+        for u in range(PACK):
+            nc.vector.tensor_copy(pb2[:, u, :], s_t[u][:].indirect(n6_l[:]))
+        nc.scalar.activation(mag[:], pb2[:].rearrange("p u w -> p (u w)"), ACT.Abs)
+        nc.scalar.activation(lg[:], mag[:], ACT.Ln, bias=half[:])
+        nc.scalar.activation(inv[:].rearrange("p u w -> p (u w)"), lg[:], ACT.Exp, scale=-1.0)
+
+        def c_gather(u):
+            nc.vector.tensor_copy(pa2[u][:], s_t[u][:].indirect(n5_l[:]))
+
+        def c_max(u):
+            nc.vector.tensor_tensor(rb2[u][:], pa2[u][:], pb2[:, u, :], ALU.max)
+
+        def c_put_max(u):
+            nc.vector.tensor_copy(y[u][:].indirect(n6_l[:]), rb2[u][:])
+
+        def c_put_ratio(u):
+            nc.vector.tensor_tensor(y[u][:].indirect(n5_l[:]), pa2[u][:], inv[:, u, :], ALU.mult)
+            nc.sync.dma_start(out=out_rows[:, u, :], in_=y[u][:])
+            if u < PACK - 1:
+                nc.scalar.copy(y_g[:, :, u], y[u][:])
+
+        c_gather(0)
+        c_gather(1)
+        c_max(0)
+        c_gather(2)
+        c_max(1)
+        c_put_max(0)
+        c_gather(3)
+        c_max(2)
+        c_put_max(1)
+        c_max(3)
+        c_put_max(2)
+        c_put_ratio(0)
+        c_put_ratio(1)
+        c_put_max(3)
+        c_put_ratio(2)
+        c_put_ratio(3)
+
+        y_c = sb("y_c", [P, V], U32)
+        y_s = sb("y_s", [P, V], U8)
+        words = out_1[0].rearrange("p n r -> p (n r)").bitcast(I32)
+        for c0 in range(0, V, 256):
+            cols = slice(c0, c0 + 256)
+            nc.scalar.copy(y_g[:, cols, PACK - 1], y[PACK - 1][:, cols])
+            nc.vector.quantize_mx(out=y_c[:, cols].bitcast(FP8X4), scales=y_s[:, cols], in_=y_g[:, cols, :].rearrange("p c t -> p (c t)"))
+            nc.sync.dma_start(out=words[:, cols], in_=y_c[:, cols].bitcast(I32))
+        rows = out_2[0].bitcast(I32)
+        for q in range(4):
+            eng = nc.scalar if q % 2 else nc.sync
+            eng.dma_start(out=rows[4 * q : 4 * q + 4, :], in_=y_s[:].bitcast(I32)[32 * q : 32 * q + 4, :])

@@ -71,13 +71,13 @@ def tile_picked_kqbondsendgratio_none_po_kernel(
             )
             return codes, sc
 
-        w2_raw = sb("w2_raw", [P, 2 * H], U8)
-        nc.sync.dma_start(out=w2_raw[:].bitcast(I32), in_=w2_words[0].bitcast(I32))
         xs = load_scales("xs", x_scales, T)
         two_l = load_list("two_l", two)
+        offs_l = load_list("offs_l", offs)
+        w2_raw = sb("w2_raw", [P, 2 * H], U8)
+        nc.sync.dma_start(out=w2_raw[:].bitcast(I32), in_=w2_words[0].bitcast(I32))
         xw = sb("xw", [P, T], I32)
         nc.sync.dma_start(out=xw[:], in_=x_words[0].rearrange("p n r -> p (n r)").bitcast(I32))
-        offs_l = load_list("offs_l", offs)
         w2_raw_s = load_scales("w2_raw_s", w2_scales, H)
         n4_l = load_list("n4_l", n4)
         n3_l = load_list("n3_l", n3)
@@ -92,11 +92,11 @@ def tile_picked_kqbondsendgratio_none_po_kernel(
         xb_s = sb("xb_s", [P, V], U8)
         xa_s = sb("xa_s", [P, S], U8)
         xb_w = sb("xb_w", [P, V], U32)
-        xa_w = sb("xa_w", [P, S], U32)
         nc.vector.tensor_copy(xb_s[:], xs[:].indirect(two_l[:]))
-        nc.vector.tensor_copy(xa_s[:], xs[:].indirect(offs_l[:]))
-        w2_c, w2_s = deal_w("w2", w2_raw, w2_raw_s)
         nc.vector.tensor_copy(xb_w[:], xw[:].bitcast(U32).indirect(two_l[:]))
+        w2_c, w2_s = deal_w("w2", w2_raw, w2_raw_s)
+        nc.vector.tensor_copy(xa_s[:], xs[:].indirect(offs_l[:]))
+        xa_w = sb("xa_w", [P, S], U32, "w2_raw_s")
         nc.vector.tensor_copy(xa_w[:], xw[:].bitcast(U32).indirect(offs_l[:]))
 
         def project(tag, codes, sc, xg_w, xg_s, t):
@@ -118,24 +118,26 @@ def tile_picked_kqbondsendgratio_none_po_kernel(
             nc.scalar.copy(b_t[t][:, :V], b_bank[t][:])
         sig = [sb(f"sig{t}", [P, V], F32) for t in range(PACK)]
         for t in range(PACK):
-            nc.scalar.activation(sig[t][:], b_bank[t][:], ACT.Sigmoid)
+            nc.scalar.activation(sig[t][:], b_t[t][:, :V], ACT.Sigmoid)
 
         bg = [sb(f"bg{t}", [P, V], F32) for t in range(PACK)]
         sm = [sb(f"sm{t}", [P, V], F32) for t in range(PACK)]
         ds2 = [sb(f"ds2_{t}", [P, 2 * V], F32) for t in range(PACK)]
-        z2_rows = sb("z2_rows", [P, PACK, V], BF16)
+        gated = [sb(f"gated{t}", [P, V], F32) for t in range(PACK)]
+        z2_g = sb("z2_g", [P, V, PACK], BF16)
 
         def b_gather(t):
             nc.vector.tensor_copy(bg[t][:], b_t[t][:].indirect(n4_l[:]))
 
         def b_max(t):
-            nc.vector.tensor_tensor(sm[t][:], bg[t][:], b_t[t][:, :V], ALU.max)
+            nc.vector.tensor_tensor(sm[t][:], bg[t][:], b_bank[t][:], ALU.max)
 
         def b_scatter(t):
             nc.vector.tensor_copy(ds2[t][:].indirect(n3_l[:]), sm[t][:])
 
         def b_gate(t):
-            nc.vector.scalar_tensor_tensor(z2_rows[:, t, :], ds2[t][:, :V], gb_t[:, t : t + 1], sig[t][:], ALU.mult, ALU.mult)
+            nc.gpsimd.tensor_tensor(gated[t][:], ds2[t][:, :V], sig[t][:], ALU.mult)
+            nc.scalar.activation(z2_g[:, :, t], gated[t][:], ACT.Copy, scale=gb_t[:, t : t + 1])
 
         pa = [sb(f"pa{t}", [P, W], F32) for t in range(PACK)]
         pb = [sb(f"pb{t}", [P, W], F32) for t in range(PACK)]
@@ -166,19 +168,14 @@ def tile_picked_kqbondsendgratio_none_po_kernel(
         b_max(2)
         b_scatter(1)
         b_max(3)
-        b_scatter(2)
         b_gate(0)
-        b_scatter(3)
+        b_scatter(2)
         b_gate(1)
+        b_scatter(3)
         b_gate(2)
-        a_gather(0)
         b_gate(3)
+        a_gather(0)
 
-        z2_g = sb("z2_g", [P, V, PACK], BF16)
-        nc.scalar.copy(
-            z2_g[:].rearrange("p (c i) t -> p c t i", i=4),
-            z2_rows[:].rearrange("p t (c i) -> p c t i", i=4),
-        )
         z_g = sb("z_g", [P, PACK, 128, PACK], BF16)
 
         def z_round(t, chunks):
@@ -212,10 +209,16 @@ def tile_picked_kqbondsendgratio_none_po_kernel(
         z_round(2, False)
         a_sum(3)
         a_prod(3)
-        z_round(3, True)
 
         s_t = [sb(f"s{u}", [P, V], F32) for u in range(PACK)]
-        for u in range(PACK):
+
+        def z_last(u):
+            t = PACK - 1
+            nc.scalar.activation(
+                z_g[:, u, :, t], dt[t][:].rearrange("p (m u) -> p u m", u=PACK)[:, u, :], ACT.Copy, scale=ga_t[:, t : t + 1]
+            )
+
+        def s_tile(u):
             z_c = sb(f"z_c{u}", [P, 128], U32)
             z_s = sb(f"z_s{u}", [P, 128], U8)
             nc.vector.quantize_mx(out=z_c[:].bitcast(FP8X4), scales=z_s[:], in_=z_g[:, u, :, :].rearrange("p m t -> p (m t)"))
@@ -230,6 +233,15 @@ def tile_picked_kqbondsendgratio_none_po_kernel(
                 stop=True,
             )
             nc.scalar.activation(s_t[u][:], bank[:], ACT.Copy, scale=0.0625)
+
+        z_last(0)
+        z_last(1)
+        z_last(2)
+        s_tile(0)
+        z_last(3)
+        s_tile(1)
+        s_tile(2)
+        s_tile(3)
 
         pa2 = [sb(f"pa2_{u}", [P, W], F32) for u in range(PACK)]
         pb2 = sb("pb2", [P, PACK, W], F32)
@@ -275,9 +287,9 @@ def tile_picked_kqbondsendgratio_none_po_kernel(
         c_put_max(1)
         c_max(3)
         c_put_max(2)
+        c_put_max(3)
         c_put_ratio(0)
         c_put_ratio(1)
-        c_put_max(3)
         c_put_ratio(2)
         c_put_ratio(3)
 

@@ -61,11 +61,11 @@ def tile_picked_kqbondsendgratio_none_po_kernel(
         def deal_w(name, raw, raw_s, tags=(None, None)):
             codes = sb(name + "_c", [P, 2 * H], U8, tags[0])
             sc = sb(name + "_s", [P, H], U8, tags[1])
-            nc.vector.tensor_copy(
+            nc.gpsimd.tensor_copy(
                 out=codes[:].bitcast(I32).rearrange("p (t q e) -> p t q e", t=PACK, e=2),
                 in_=raw[:].bitcast(I32).rearrange("p (q t e) -> p t q e", t=PACK, e=2),
             )
-            nc.vector.tensor_copy(
+            nc.gpsimd.tensor_copy(
                 out=sc[:].bitcast(I32).rearrange("p (t q) -> p t q", t=PACK),
                 in_=raw_s[:].bitcast(I32).rearrange("p (q t) -> p t q", t=PACK),
             )
@@ -96,7 +96,7 @@ def tile_picked_kqbondsendgratio_none_po_kernel(
         nc.vector.tensor_copy(xb_w[:], xw[:].bitcast(U32).indirect(two_l[:]))
         w2_c, w2_s = deal_w("w2", w2_raw, w2_raw_s)
         nc.vector.tensor_copy(xa_s[:], xs[:].indirect(offs_l[:]))
-        xa_w = sb("xa_w", [P, S], U32, "w2_raw_s")
+        xa_w = sb("xa_w", [P, S], U32)
         nc.vector.tensor_copy(xa_w[:], xw[:].bitcast(U32).indirect(offs_l[:]))
 
         def project(tag, codes, sc, xg_w, xg_s, t):
@@ -139,19 +139,20 @@ def tile_picked_kqbondsendgratio_none_po_kernel(
             nc.gpsimd.tensor_tensor(gated[t][:], ds2[t][:, :V], sig[t][:], ALU.mult)
             nc.scalar.activation(z2_g[:, :, t], gated[t][:], ACT.Copy, scale=gb_t[:, t : t + 1])
 
-        pa = [sb(f"pa{t}", [P, W], F32) for t in range(PACK)]
-        pb = [sb(f"pb{t}", [P, W], F32) for t in range(PACK)]
+        pab = {}
         dt = [sb(f"dt{t}", [P, S], F32) for t in range(PACK)]
 
         def a_gather(t):
-            nc.vector.tensor_copy(pa[t][:], a_t[t][:].indirect(n1_l[:]))
-            nc.vector.tensor_copy(pb[t][:], a_t[t][:].indirect(n2_l[:]))
+            if t % 2 == 0:
+                pab[t // 2] = sb(f"pab{t // 2}", [P, 2, 2, W], F32, "sm2" if t == 0 else None)
+            nc.vector.tensor_copy(pab[t // 2][:, t % 2, 0, :], a_t[t][:].indirect(n1_l[:]))
+            nc.vector.tensor_copy(pab[t // 2][:, t % 2, 1, :], a_t[t][:].indirect(n2_l[:]))
 
         def a_sum(t):
-            nc.vector.tensor_tensor(dt[t][:].indirect(n1_l[:]), pa[t][:], pb[t][:], ALU.add)
+            nc.vector.tensor_tensor(dt[t][:].indirect(n1_l[:]), pab[t // 2][:, t % 2, 0, :], pab[t // 2][:, t % 2, 1, :], ALU.add)
 
         def a_prod(t):
-            nc.vector.tensor_tensor(dt[t][:].indirect(n2_l[:]), pa[t][:], pb[t][:], ALU.mult)
+            nc.vector.tensor_tensor(dt[t][:].indirect(n2_l[:]), pab[t // 2][:, t % 2, 0, :], pab[t // 2][:, t % 2, 1, :], ALU.mult)
 
         b_gather(0)
         b_gather(1)
@@ -159,7 +160,7 @@ def tile_picked_kqbondsendgratio_none_po_kernel(
         b_gather(2)
         b_max(1)
         b_scatter(0)
-        w1_c, w1_s = deal_w("w1", w1_raw, w1_raw_s, ("bg0", "bg1"))
+        w1_c, w1_s = deal_w("w1", w1_raw, w1_raw_s)
         a_bank = [project("banka", w1_c, w1_s, xa_w, xa_s, t) for t in range(PACK)]
         a_t = [sb(f"a{t}", [P, S], F32) for t in range(PACK)]
         for t in range(PACK):
@@ -176,7 +177,7 @@ def tile_picked_kqbondsendgratio_none_po_kernel(
         b_gate(3)
         a_gather(0)
 
-        z_g = sb("z_g", [P, PACK, 128, PACK], BF16)
+        z_g = sb("z_g", [P, PACK, 128, PACK], BF16, "gated3")
 
         def z_round(t, chunks):
             if chunks:
@@ -202,13 +203,13 @@ def tile_picked_kqbondsendgratio_none_po_kernel(
         a_gather(2)
         a_prod(1)
         z_round(1, False)
-        nc.vector.quantize_mx(out=z2_c[:].bitcast(FP8X4), scales=z2_s[:], in_=z2_g[:].rearrange("p c t -> p (c t)"))
-        a_sum(2)
         a_gather(3)
+        a_sum(2)
+        a_sum(3)
         a_prod(2)
         z_round(2, False)
-        a_sum(3)
         a_prod(3)
+        nc.vector.quantize_mx(out=z2_c[:].bitcast(FP8X4), scales=z2_s[:], in_=z2_g[:].rearrange("p c t -> p (c t)"))
 
         s_t = [sb(f"s{u}", [P, V], F32) for u in range(PACK)]
 
@@ -222,17 +223,24 @@ def tile_picked_kqbondsendgratio_none_po_kernel(
             z_c = sb(f"z_c{u}", [P, 128], U32)
             z_s = sb(f"z_s{u}", [P, 128], U8)
             nc.vector.quantize_mx(out=z_c[:].bitcast(FP8X4), scales=z_s[:], in_=z_g[:, u, :, :].rearrange("p m t -> p (m t)"))
-            bank = psum.tile([P, 512], F32, name=f"s_bank{u}", tag=f"bankb{u}")
-            nc.tensor.matmul_mx(
-                out=bank[:],
-                lhsT=z_c[:].bitcast(FP8X4),
-                lhsT_scale=z_s[:],
-                rhs=z2_c[:].bitcast(FP8X4),
-                rhs_scale=z2_s[:],
-                start=True,
-                stop=True,
-            )
-            nc.scalar.activation(s_t[u][:], bank[:], ACT.Copy, scale=0.0625)
+            parts = 2 if u == 0 else 1
+            width = V // parts
+            for h in range(parts):
+                cols = slice(h * width, (h + 1) * width)
+                bank = psum.tile([P, width], F32, name=f"s_bank{u}_{h}", tag=("bankb", "banka")[h] + str(u))
+                nc.tensor.matmul_mx(
+                    out=bank[:],
+                    lhsT=z_c[:].bitcast(FP8X4),
+                    lhsT_scale=z_s[:],
+                    rhs=z2_c[:, cols].bitcast(FP8X4),
+                    rhs_scale=z2_s[:, cols],
+                    start=True,
+                    stop=True,
+                )
+                if h == 0:
+                    nc.scalar.activation(s_t[u][:, cols], bank[:], ACT.Copy, scale=0.0625)
+                else:
+                    nc.vector.tensor_scalar(s_t[u][:, cols], bank[:], 0.0625, None, ALU.mult)
 
         z_last(0)
         z_last(1)
@@ -273,8 +281,10 @@ def tile_picked_kqbondsendgratio_none_po_kernel(
         def c_put_ratio(u):
             nc.vector.tensor_tensor(y[u][:].indirect(n5_l[:]), pa2[u][:], inv[:, u, :], ALU.mult)
             nc.sync.dma_start(out=out_rows[:, u, :], in_=y[u][:])
-            if u < PACK - 1:
+            if u < PACK - 2:
                 nc.scalar.copy(y_g[:, :, u], y[u][:])
+            elif u == PACK - 2:
+                nc.scalar.copy(y_g[:, :, u : u + 2], y[u][:].unsqueeze(2).to_broadcast([P, V, 2]))
 
         c_gather(0)
         c_gather(1)
@@ -288,9 +298,9 @@ def tile_picked_kqbondsendgratio_none_po_kernel(
         c_max(3)
         c_put_max(2)
         c_put_max(3)
+        c_put_ratio(2)
         c_put_ratio(0)
         c_put_ratio(1)
-        c_put_ratio(2)
         c_put_ratio(3)
 
         y_c = sb("y_c", [P, V], U32)
@@ -298,7 +308,9 @@ def tile_picked_kqbondsendgratio_none_po_kernel(
         words = out_1[0].rearrange("p n r -> p (n r)").bitcast(I32)
         for c0 in range(0, V, 256):
             cols = slice(c0, c0 + 256)
-            nc.scalar.copy(y_g[:, cols, PACK - 1], y[PACK - 1][:, cols])
+            nc.vector.tensor_copy(y_g[:, cols, PACK - 1], y[PACK - 1][:, cols])
+        for c0 in range(0, V, 256):
+            cols = slice(c0, c0 + 256)
             nc.vector.quantize_mx(out=y_c[:, cols].bitcast(FP8X4), scales=y_s[:, cols], in_=y_g[:, cols, :].rearrange("p c t -> p (c t)"))
             nc.sync.dma_start(out=words[:, cols], in_=y_c[:, cols].bitcast(I32))
         rows = out_2[0].bitcast(I32)

@@ -99,23 +99,25 @@ def tile_picked_kqbondsendgratio_none_po_kernel(
         xa_w = sb("xa_w", [P, S], U32)
         nc.vector.tensor_copy(xa_w[:], xw[:].bitcast(U32).indirect(offs_l[:]))
 
-        def project(tag, codes, sc, xg_w, xg_s, t):
-            bank = psum.tile([P, 512], F32, name=f"{tag}{t}", tag=f"{tag}{t}")
+        def project(tag, codes, sc, xg_w, xg_s, t, cols=slice(0, 512)):
+            bank = psum.tile([P, cols.stop - cols.start], F32, name=f"proj_{tag}_{t}", tag=tag)
             nc.tensor.matmul_mx(
                 out=bank[:],
                 lhsT=codes[:, 256 * t : 256 * (t + 1)].bitcast(FP4X4),
                 lhsT_scale=sc[:, 128 * t : 128 * (t + 1)],
-                rhs=xg_w[:].bitcast(FP8X4),
-                rhs_scale=xg_s[:],
+                rhs=xg_w[:, cols].bitcast(FP8X4),
+                rhs_scale=xg_s[:, cols],
                 start=True,
                 stop=True,
             )
-            return bank
+            return bank, cols
 
-        b_bank = [project("bankb", w2_c, w2_s, xb_w, xb_s, t) for t in range(PACK)]
+        b_bank = [[project("bankb0", w2_c, w2_s, xb_w, xb_s, 0, slice(0, 256)), project("banka3", w2_c, w2_s, xb_w, xb_s, 0, slice(256, 512))]]
+        b_bank = b_bank + [[project(f"bankb{t}", w2_c, w2_s, xb_w, xb_s, t)] for t in range(1, PACK)]
         b_t = [sb(f"b{t}", [P, 2 * V], F32) for t in range(PACK)]
         for t in range(PACK):
-            nc.scalar.copy(b_t[t][:, :V], b_bank[t][:])
+            for bank, cols in b_bank[t]:
+                nc.scalar.copy(b_t[t][:, cols], bank[:])
         sig = [sb(f"sig{t}", [P, V], F32) for t in range(PACK)]
         for t in range(PACK):
             nc.scalar.activation(sig[t][:], b_t[t][:, :V], ACT.Sigmoid)
@@ -130,7 +132,8 @@ def tile_picked_kqbondsendgratio_none_po_kernel(
             nc.vector.tensor_copy(bg[t][:], b_t[t][:].indirect(n4_l[:]))
 
         def b_max(t):
-            nc.vector.tensor_tensor(sm[t][:], bg[t][:], b_bank[t][:], ALU.max)
+            for bank, cols in b_bank[t]:
+                nc.vector.tensor_tensor(sm[t][:, cols], bg[t][:, cols], bank[:], ALU.max)
 
         def b_scatter(t):
             nc.vector.tensor_copy(ds2[t][:].indirect(n3_l[:]), sm[t][:])
@@ -161,7 +164,7 @@ def tile_picked_kqbondsendgratio_none_po_kernel(
         b_max(1)
         b_scatter(0)
         w1_c, w1_s = deal_w("w1", w1_raw, w1_raw_s)
-        a_bank = [project("banka", w1_c, w1_s, xa_w, xa_s, t) for t in range(PACK)]
+        a_bank = [project(f"banka{t}", w1_c, w1_s, xa_w, xa_s, t)[0] for t in range(PACK)]
         a_t = [sb(f"a{t}", [P, S], F32) for t in range(PACK)]
         for t in range(PACK):
             nc.scalar.copy(a_t[t][:], a_bank[t][:])
@@ -179,19 +182,17 @@ def tile_picked_kqbondsendgratio_none_po_kernel(
 
         z_g = sb("z_g", [P, PACK, 128, PACK], BF16, "gated3")
 
-        def z_round(t, chunks):
-            if chunks:
-                for u in range(PACK):
-                    nc.scalar.activation(
-                        z_g[:, u, :, t], dt[t][:].rearrange("p (m u) -> p u m", u=PACK)[:, u, :], ACT.Copy, scale=ga_t[:, t : t + 1]
-                    )
-            else:
+        def z_round(t):
+            src = dt[t][:].rearrange("p (m u) -> p m u", u=PACK)
+            if t == PACK - 2:
                 nc.scalar.activation(
-                    z_g[:, :, :, t].rearrange("p u m -> p m u"),
-                    dt[t][:].rearrange("p (m u) -> p m u", u=PACK),
+                    z_g[:, :, :, t : t + 2].rearrange("p u m e -> p m u e"),
+                    src.unsqueeze(3).to_broadcast([P, 128, PACK, 2]),
                     ACT.Copy,
                     scale=ga_t[:, t : t + 1],
                 )
+            else:
+                nc.scalar.activation(z_g[:, :, :, t].rearrange("p u m -> p m u"), src, ACT.Copy, scale=ga_t[:, t : t + 1])
 
         z2_c = sb("z2_c", [P, V], U32)
         z2_s = sb("z2_s", [P, V], U8)
@@ -199,15 +200,15 @@ def tile_picked_kqbondsendgratio_none_po_kernel(
         a_sum(0)
         a_sum(1)
         a_prod(0)
-        z_round(0, False)
+        z_round(0)
         a_gather(2)
         a_prod(1)
-        z_round(1, False)
+        z_round(1)
         a_gather(3)
         a_sum(2)
         a_sum(3)
         a_prod(2)
-        z_round(2, False)
+        z_round(2)
         a_prod(3)
         nc.vector.quantize_mx(out=z2_c[:].bitcast(FP8X4), scales=z2_s[:], in_=z2_g[:].rearrange("p c t -> p (c t)"))
 
@@ -215,9 +216,11 @@ def tile_picked_kqbondsendgratio_none_po_kernel(
 
         def z_last(u):
             t = PACK - 1
-            nc.scalar.activation(
-                z_g[:, u, :, t], dt[t][:].rearrange("p (m u) -> p u m", u=PACK)[:, u, :], ACT.Copy, scale=ga_t[:, t : t + 1]
-            )
+            src = dt[t][:].rearrange("p (m u) -> p u m", u=PACK)[:, u, :]
+            if u < 2:
+                nc.scalar.activation(z_g[:, u, :, t], src, ACT.Copy, scale=ga_t[:, t : t + 1])
+            else:
+                nc.vector.tensor_scalar(z_g[:, u, :, t], src, ga_t[:, t : t + 1], None, ALU.mult)
 
         def s_tile(u):
             z_c = sb(f"z_c{u}", [P, 128], U32)
@@ -237,23 +240,20 @@ def tile_picked_kqbondsendgratio_none_po_kernel(
                     start=True,
                     stop=True,
                 )
-                if h == 0:
-                    nc.scalar.activation(s_t[u][:, cols], bank[:], ACT.Copy, scale=0.0625)
-                else:
-                    nc.vector.tensor_scalar(s_t[u][:, cols], bank[:], 0.0625, None, ALU.mult)
+                nc.scalar.activation(s_t[u][:, cols], bank[:], ACT.Copy, scale=0.0625)
 
         z_last(0)
         z_last(1)
-        z_last(2)
         s_tile(0)
-        z_last(3)
+        z_last(2)
         s_tile(1)
+        z_last(3)
         s_tile(2)
         s_tile(3)
 
-        pa2 = [sb(f"pa2_{u}", [P, W], F32) for u in range(PACK)]
+        pa2 = sb("pa2", [P, PACK, W], F32)
         pb2 = sb("pb2", [P, PACK, W], F32)
-        rb2 = [sb(f"rb2_{u}", [P, W], F32) for u in range(PACK)]
+        rb2 = sb("rb2", [P, PACK, W], F32)
         y = [sb(f"y{u}", [P, V], F32) for u in range(PACK)]
         mag = sb("mag", [P, PACK * W], F32)
         lg = sb("lg", [P, PACK * W], F32)
@@ -270,16 +270,16 @@ def tile_picked_kqbondsendgratio_none_po_kernel(
         nc.scalar.activation(inv[:].rearrange("p u w -> p (u w)"), lg[:], ACT.Exp, scale=-1.0)
 
         def c_gather(u):
-            nc.vector.tensor_copy(pa2[u][:], s_t[u][:].indirect(n5_l[:]))
+            nc.vector.tensor_copy(pa2[:, u, :], s_t[u][:].indirect(n5_l[:]))
 
         def c_max(u):
-            nc.vector.tensor_tensor(rb2[u][:], pa2[u][:], pb2[:, u, :], ALU.max)
+            nc.vector.tensor_tensor(rb2[:, u : u + 2, :], pa2[:, u : u + 2, :], pb2[:, u : u + 2, :], ALU.max)
 
         def c_put_max(u):
-            nc.vector.tensor_copy(y[u][:].indirect(n6_l[:]), rb2[u][:])
+            nc.vector.tensor_copy(y[u][:].indirect(n6_l[:]), rb2[:, u, :])
 
         def c_put_ratio(u):
-            nc.vector.tensor_tensor(y[u][:].indirect(n5_l[:]), pa2[u][:], inv[:, u, :], ALU.mult)
+            nc.vector.tensor_tensor(y[u][:].indirect(n5_l[:]), pa2[:, u, :], inv[:, u, :], ALU.mult)
             nc.sync.dma_start(out=out_rows[:, u, :], in_=y[u][:])
             if u < PACK - 2:
                 nc.scalar.copy(y_g[:, :, u], y[u][:])
@@ -288,14 +288,12 @@ def tile_picked_kqbondsendgratio_none_po_kernel(
 
         c_gather(0)
         c_gather(1)
-        c_max(0)
         c_gather(2)
-        c_max(1)
-        c_put_max(0)
+        c_max(0)
         c_gather(3)
+        c_put_max(0)
         c_max(2)
         c_put_max(1)
-        c_max(3)
         c_put_max(2)
         c_put_max(3)
         c_put_ratio(2)
@@ -306,9 +304,9 @@ def tile_picked_kqbondsendgratio_none_po_kernel(
         y_c = sb("y_c", [P, V], U32)
         y_s = sb("y_s", [P, V], U8)
         words = out_1[0].rearrange("p n r -> p (n r)").bitcast(I32)
-        for c0 in range(0, V, 256):
-            cols = slice(c0, c0 + 256)
-            nc.vector.tensor_copy(y_g[:, cols, PACK - 1], y[PACK - 1][:, cols])
+        nc.vector.tensor_copy(y_g[:, 0:256, PACK - 1], y[PACK - 1][:, 0:256])
+        nc.vector.tensor_copy(y_g[:, 256:384, PACK - 1], y[PACK - 1][:, 256:384])
+        nc.scalar.copy(y_g[:, 384:512, PACK - 1], y[PACK - 1][:, 384:512])
         for c0 in range(0, V, 256):
             cols = slice(c0, c0 + 256)
             nc.vector.quantize_mx(out=y_c[:, cols].bitcast(FP8X4), scales=y_s[:, cols], in_=y_g[:, cols, :].rearrange("p c t -> p (c t)"))

@@ -2,7 +2,7 @@ from contextlib import ExitStack
 
 import concourse.mybir as mybir
 
-K, T, S, V, H, W = 512, 2048, 512, 512, 512, 256
+T, S, V, H, W = 2048, 512, 512, 512, 256
 FLOPS = 3 * 2 * 512 * 512 * 512
 
 F32 = mybir.dt.float32
@@ -17,7 +17,12 @@ ALU = mybir.AluOpType
 ACT = mybir.ActivationFunctionType
 
 P = 128
-PACK = 4
+TILES = 4
+LAST = TILES - 1
+QUADS = 4
+HALF = 256
+QUARTER = 128
+SCALAR_PARTS = 2
 
 
 def tile_picked_kqbondsendgratio_none_po_kernel(
@@ -28,60 +33,59 @@ def tile_picked_kqbondsendgratio_none_po_kernel(
         keep = ctx.enter_context(tc.tile_pool(name="keep", bufs=1))
         psum = ctx.enter_context(tc.psum_pool(name="psum", bufs=1))
 
-        def sb(name, shape, dtype, tag=None):
+        def sbuf(name, shape, dtype, tag=None):
             return keep.tile(shape, dtype, name=name, tag=tag or name, align_bytes=64)
 
         def load_list(name, src):
-            t = keep.tile(list(src.shape), U16, name=name)
-            nc.sync.dma_start(t[:], src)
-            return t
+            tile = keep.tile(list(src.shape), U16, name=name)
+            nc.sync.dma_start(tile[:], src)
+            return tile
 
-        def load_scales(name, src, width):
-            t = sb(name, [P, width], U8)
-            nc.vector.memset(t[:].bitcast(I32), 0)
+        def load_scales(name, src, width, queues):
+            tile = sbuf(name, [P, width], U8)
+            nc.vector.memset(tile[:].bitcast(I32), 0)
             rows = src[0].bitcast(I32)
-            for q in range(4):
-                nc.sync.dma_start(out=t[:].bitcast(I32)[32 * q : 32 * q + 4, :], in_=rows[4 * q : 4 * q + 4, :])
-            return t
+            for q in range(QUADS):
+                queues[q % len(queues)].dma_start(out=tile[:].bitcast(I32)[32 * q : 32 * q + 4, :], in_=rows[4 * q : 4 * q + 4, :])
+            return tile
+
+        def load_fp4_words(name, words):
+            tile = sbuf(name, [P, 2 * H], U8)
+            nc.sync.dma_start(out=tile[:].bitcast(I32), in_=words[0].bitcast(I32))
+            return tile
 
         def load_gain(name, src):
-            t = sb(name, [P, PACK], F32)
-            view = src.rearrange("(q t i) o -> i q (t o)", t=PACK, i=4)
-            with nc.allow_non_contiguous_dma(reason="one value a row"):
+            gain = sbuf(name, [P, TILES], F32)
+            view = src.rearrange("(q t i) o -> i q (t o)", t=TILES, i=4)
+            with nc.allow_non_contiguous_dma(reason="one value for each feature"):
                 for i in range(4):
-                    nc.sync.dma_start(out=t[i:P:4, :], in_=view[i])
-            return t
+                    nc.sync.dma_start(out=gain[i:P:4, :], in_=view[i])
+            return gain
 
-        def load_w(name, words, scales):
-            raw = sb(name + "_raw", [P, 2 * H], U8)
-            nc.sync.dma_start(out=raw[:].bitcast(I32), in_=words[0].bitcast(I32))
-            raw_s = load_scales(name + "_raw_s", scales, H)
-            return raw, raw_s
-
-        def deal_w(name, raw, raw_s, tags=(None, None)):
-            codes = sb(name + "_c", [P, 2 * H], U8, tags[0])
-            sc = sb(name + "_s", [P, H], U8, tags[1])
+        def deal_weight(name, words, scales):
+            dealt_words = sbuf(name + "_dealt_words", [P, 2 * H], U8)
+            dealt_scales = sbuf(name + "_dealt_scales", [P, H], U8)
             nc.gpsimd.tensor_copy(
-                out=codes[:].bitcast(I32).rearrange("p (t q e) -> p t q e", t=PACK, e=2),
-                in_=raw[:].bitcast(I32).rearrange("p (q t e) -> p t q e", t=PACK, e=2),
+                out=dealt_words[:].bitcast(I32).rearrange("p (t q e) -> p t q e", t=TILES, e=2),
+                in_=words[:].bitcast(I32).rearrange("p (q t e) -> p t q e", t=TILES, e=2),
             )
             nc.gpsimd.tensor_copy(
-                out=sc[:].bitcast(I32).rearrange("p (t q) -> p t q", t=PACK),
-                in_=raw_s[:].bitcast(I32).rearrange("p (q t) -> p t q", t=PACK),
+                out=dealt_scales[:].bitcast(I32).rearrange("p (t q) -> p t q", t=TILES),
+                in_=scales[:].bitcast(I32).rearrange("p (q t) -> p t q", t=TILES),
             )
-            return codes, sc
+            return dealt_words, dealt_scales
 
-        xs = load_scales("xs", x_scales, T)
+        xs = load_scales("xs", x_scales, T, (nc.sync, nc.scalar))
         two_l = load_list("two_l", two)
         offs_l = load_list("offs_l", offs)
-        w2_raw = sb("w2_raw", [P, 2 * H], U8)
-        nc.sync.dma_start(out=w2_raw[:].bitcast(I32), in_=w2_words[0].bitcast(I32))
-        xw = sb("xw", [P, T], I32)
+        w2_raw = load_fp4_words("w2_raw", w2_words)
+        xw = sbuf("xw", [P, T], I32)
         nc.sync.dma_start(out=xw[:], in_=x_words[0].rearrange("p n r -> p (n r)").bitcast(I32))
-        w2_raw_s = load_scales("w2_raw_s", w2_scales, H)
+        w2_raw_s = load_scales("w2_raw_s", w2_scales, H, (nc.sync,))
         n4_l = load_list("n4_l", n4)
         n3_l = load_list("n3_l", n3)
-        w1_raw, w1_raw_s = load_w("w1", w1_words, w1_scales)
+        w1_raw = load_fp4_words("w1_raw", w1_words)
+        w1_raw_s = load_scales("w1_raw_s", w1_scales, H, (nc.sync,))
         n1_l = load_list("n1_l", n1)
         n2_l = load_list("n2_l", n2)
         gb_t = load_gain("gb_t", gb)
@@ -89,73 +93,63 @@ def tile_picked_kqbondsendgratio_none_po_kernel(
         n5_l = load_list("n5_l", n5)
         n6_l = load_list("n6_l", n6)
 
-        xb_s = sb("xb_s", [P, V], U8)
-        xa_s = sb("xa_s", [P, S], U8)
-        xb_w = sb("xb_w", [P, V], U32)
+        xb_s = sbuf("xb_s", [P, V], U8)
+        xa_s = sbuf("xa_s", [P, S], U8)
+        xb_w = sbuf("xb_w", [P, V], U32)
         nc.vector.tensor_copy(xb_s[:], xs[:].indirect(two_l[:]))
         nc.vector.tensor_copy(xb_w[:], xw[:].bitcast(U32).indirect(two_l[:]))
-        w2_c, w2_s = deal_w("w2", w2_raw, w2_raw_s)
+        w2_w, w2_s = deal_weight("w2", w2_raw, w2_raw_s)
         nc.vector.tensor_copy(xa_s[:], xs[:].indirect(offs_l[:]))
-        xa_w = sb("xa_w", [P, S], U32)
+        xa_w = sbuf("xa_w", [P, S], U32)
         nc.vector.tensor_copy(xa_w[:], xw[:].bitcast(U32).indirect(offs_l[:]))
 
-        def project(tag, codes, sc, xg_w, xg_s, t, cols=slice(0, 512)):
+        def project(tag, w_w, w_s, x_w, x_s, t, cols):
             bank = psum.tile([P, cols.stop - cols.start], F32, name=f"proj_{tag}_{t}", tag=tag)
             nc.tensor.matmul_mx(
                 out=bank[:],
-                lhsT=codes[:, 256 * t : 256 * (t + 1)].bitcast(FP4X4),
-                lhsT_scale=sc[:, 128 * t : 128 * (t + 1)],
-                rhs=xg_w[:, cols].bitcast(FP8X4),
-                rhs_scale=xg_s[:, cols],
+                lhsT=w_w[:, 2 * P * t : 2 * P * (t + 1)].bitcast(FP4X4),
+                lhsT_scale=w_s[:, P * t : P * (t + 1)],
+                rhs=x_w[:, cols].bitcast(FP8X4),
+                rhs_scale=x_s[:, cols],
                 start=True,
                 stop=True,
             )
-            return bank, cols
+            return bank
 
-        b_bank = [[project("bankb0", w2_c, w2_s, xb_w, xb_s, 0, slice(0, 256)), project("banka3", w2_c, w2_s, xb_w, xb_s, 0, slice(256, 512))]]
-        b_bank = b_bank + [[project(f"bankb{t}", w2_c, w2_s, xb_w, xb_s, t)] for t in range(1, PACK)]
-        b_t = [sb(f"b{t}", [P, 2 * V], F32) for t in range(PACK)]
-        for t in range(PACK):
-            for bank, cols in b_bank[t]:
-                nc.scalar.copy(b_t[t][:, cols], bank[:])
-        sig = [sb(f"sig{t}", [P, V], F32) for t in range(PACK)]
-        for t in range(PACK):
-            nc.scalar.activation(sig[t][:], b_t[t][:, :V], ACT.Sigmoid)
+        whole = slice(0, V)
+        halves = (slice(0, HALF), slice(HALF, V))
+        b_parts = [[("bank_b0", halves[0]), ("bank_a3", halves[1])]] + [[(f"bank_b{t}", whole)] for t in range(1, TILES)]
+        b_banks = [[(project(tag, w2_w, w2_s, xb_w, xb_s, t, cols), cols) for tag, cols in b_parts[t]] for t in range(TILES)]
 
-        bg = [sb(f"bg{t}", [P, V], F32) for t in range(PACK)]
-        sm = [sb(f"sm{t}", [P, V], F32) for t in range(PACK)]
-        ds2 = [sb(f"ds2_{t}", [P, 2 * V], F32) for t in range(PACK)]
-        gated = [sb(f"gated{t}", [P, V], F32) for t in range(PACK)]
-        z2_g = sb("z2_g", [P, V, PACK], BF16)
+        b = [sbuf(f"b{t}", [P, 2 * V], F32) for t in range(TILES)]
+        for t in range(TILES):
+            for bank, cols in b_banks[t]:
+                nc.scalar.copy(b[t][:, cols], bank[:])
+        sig = [sbuf(f"sig{t}", [P, V], F32) for t in range(TILES)]
+        for t in range(TILES):
+            nc.scalar.activation(sig[t][:], b[t][:, :V], ACT.Sigmoid)
+
+        b_n4 = [sbuf(f"b_n4_{t}", [P, V], F32) for t in range(TILES)]
+        sm = [sbuf(f"sm{t}", [P, V], F32) for t in range(TILES)]
+        ds2 = [sbuf(f"ds2_{t}", [P, 2 * V], F32) for t in range(TILES)]
+        gated = [sbuf(f"gated{t}", [P, V], F32) for t in range(TILES)]
+        z2_bf = sbuf("z2_bf", [P, V, TILES], BF16)
 
         def b_gather(t):
-            nc.vector.tensor_copy(bg[t][:], b_t[t][:].indirect(n4_l[:]))
+            nc.vector.tensor_copy(b_n4[t][:], b[t][:].indirect(n4_l[:]))
 
         def b_max(t):
-            for bank, cols in b_bank[t]:
-                nc.vector.tensor_tensor(sm[t][:, cols], bg[t][:, cols], bank[:], ALU.max)
+            for bank, cols in b_banks[t]:
+                nc.vector.tensor_tensor(sm[t][:, cols], b_n4[t][:, cols], bank[:], ALU.max)
 
         def b_scatter(t):
             nc.vector.tensor_copy(ds2[t][:].indirect(n3_l[:]), sm[t][:])
 
         def b_gate(t):
             nc.gpsimd.tensor_tensor(gated[t][:], ds2[t][:, :V], sig[t][:], ALU.mult)
-            nc.scalar.activation(z2_g[:, :, t], gated[t][:], ACT.Copy, scale=gb_t[:, t : t + 1])
+            nc.scalar.activation(z2_bf[:, :, t], gated[t][:], ACT.Copy, scale=gb_t[:, t : t + 1])
 
-        pab = {}
-        dt = [sb(f"dt{t}", [P, S], F32) for t in range(PACK)]
-
-        def a_gather(t):
-            if t % 2 == 0:
-                pab[t // 2] = sb(f"pab{t // 2}", [P, 2, 2, W], F32, "sm2" if t == 0 else None)
-            nc.vector.tensor_copy(pab[t // 2][:, t % 2, 0, :], a_t[t][:].indirect(n1_l[:]))
-            nc.vector.tensor_copy(pab[t // 2][:, t % 2, 1, :], a_t[t][:].indirect(n2_l[:]))
-
-        def a_sum(t):
-            nc.vector.tensor_tensor(dt[t][:].indirect(n1_l[:]), pab[t // 2][:, t % 2, 0, :], pab[t // 2][:, t % 2, 1, :], ALU.add)
-
-        def a_prod(t):
-            nc.vector.tensor_tensor(dt[t][:].indirect(n2_l[:]), pab[t // 2][:, t % 2, 0, :], pab[t // 2][:, t % 2, 1, :], ALU.mult)
+        dt = [sbuf(f"dt{t}", [P, S], F32) for t in range(TILES)]
 
         b_gather(0)
         b_gather(1)
@@ -163,11 +157,11 @@ def tile_picked_kqbondsendgratio_none_po_kernel(
         b_gather(2)
         b_max(1)
         b_scatter(0)
-        w1_c, w1_s = deal_w("w1", w1_raw, w1_raw_s)
-        a_bank = [project(f"banka{t}", w1_c, w1_s, xa_w, xa_s, t)[0] for t in range(PACK)]
-        a_t = [sb(f"a{t}", [P, S], F32) for t in range(PACK)]
-        for t in range(PACK):
-            nc.scalar.copy(a_t[t][:], a_bank[t][:])
+        w1_w, w1_s = deal_weight("w1", w1_raw, w1_raw_s)
+        a_banks = [project(f"bank_a{t}", w1_w, w1_s, xa_w, xa_s, t, whole) for t in range(TILES)]
+        a = [sbuf(f"a{t}", [P, S], F32) for t in range(TILES)]
+        for t in range(TILES):
+            nc.scalar.copy(a[t][:], a_banks[t][:])
         b_gather(3)
         b_max(2)
         b_scatter(1)
@@ -178,140 +172,148 @@ def tile_picked_kqbondsendgratio_none_po_kernel(
         b_scatter(3)
         b_gate(2)
         b_gate(3)
+
+        pab = {}
+
+        def a_gather(t):
+            if t % 2 == 0:
+                pab[t // 2] = sbuf(f"pab{t // 2}", [P, 2, 2, W], F32, "sm2" if t == 0 else None)
+            nc.vector.tensor_copy(pab[t // 2][:, t % 2, 0, :], a[t][:].indirect(n1_l[:]))
+            nc.vector.tensor_copy(pab[t // 2][:, t % 2, 1, :], a[t][:].indirect(n2_l[:]))
+
+        def a_put_sum(t):
+            nc.vector.tensor_tensor(dt[t][:].indirect(n1_l[:]), pab[t // 2][:, t % 2, 0, :], pab[t // 2][:, t % 2, 1, :], ALU.add)
+
+        def a_put_product(t):
+            nc.vector.tensor_tensor(dt[t][:].indirect(n2_l[:]), pab[t // 2][:, t % 2, 0, :], pab[t // 2][:, t % 2, 1, :], ALU.mult)
+
         a_gather(0)
 
-        z_g = sb("z_g", [P, PACK, 128, PACK], BF16, "gated3")
+        z_bf = sbuf("z_bf", [P, TILES, P, TILES], BF16, "gated3")
 
         def z_round(t):
-            src = dt[t][:].rearrange("p (m u) -> p m u", u=PACK)
-            if t == PACK - 2:
+            src = dt[t][:].rearrange("p (m u) -> p m u", u=TILES)
+            if t == LAST - 1:
                 nc.scalar.activation(
-                    z_g[:, :, :, t : t + 2].rearrange("p u m e -> p m u e"),
-                    src.unsqueeze(3).to_broadcast([P, 128, PACK, 2]),
+                    z_bf[:, :, :, t : t + 2].rearrange("p u m e -> p m u e"),
+                    src.unsqueeze(3).to_broadcast([P, P, TILES, 2]),
                     ACT.Copy,
                     scale=ga_t[:, t : t + 1],
                 )
             else:
-                nc.scalar.activation(z_g[:, :, :, t].rearrange("p u m -> p m u"), src, ACT.Copy, scale=ga_t[:, t : t + 1])
+                nc.scalar.activation(z_bf[:, :, :, t].rearrange("p u m -> p m u"), src, ACT.Copy, scale=ga_t[:, t : t + 1])
 
-        z2_c = sb("z2_c", [P, V], U32)
-        z2_s = sb("z2_s", [P, V], U8)
+        z2_w = sbuf("z2_w", [P, V], U32)
+        z2_s = sbuf("z2_s", [P, V], U8)
         a_gather(1)
-        a_sum(0)
-        a_sum(1)
-        a_prod(0)
+        a_put_sum(0)
+        a_put_sum(1)
+        a_put_product(0)
         z_round(0)
         a_gather(2)
-        a_prod(1)
+        a_put_product(1)
         z_round(1)
         a_gather(3)
-        a_sum(2)
-        a_sum(3)
-        a_prod(2)
+        a_put_sum(2)
+        a_put_sum(3)
+        a_put_product(2)
         z_round(2)
-        a_prod(3)
-        nc.vector.quantize_mx(out=z2_c[:].bitcast(FP8X4), scales=z2_s[:], in_=z2_g[:].rearrange("p c t -> p (c t)"))
+        a_put_product(3)
+        nc.vector.quantize_mx(out=z2_w[:].bitcast(FP8X4), scales=z2_s[:], in_=z2_bf[:].rearrange("p v t -> p (v t)"))
 
-        s_t = [sb(f"s{u}", [P, V], F32) for u in range(PACK)]
+        s = [sbuf(f"s{u}", [P, V], F32) for u in range(TILES)]
 
-        def z_last(u):
-            t = PACK - 1
-            src = dt[t][:].rearrange("p (m u) -> p u m", u=PACK)[:, u, :]
-            if u < 2:
-                nc.scalar.activation(z_g[:, u, :, t], src, ACT.Copy, scale=ga_t[:, t : t + 1])
+        def z_round_last(u):
+            src = dt[LAST][:].rearrange("p (m u) -> p u m", u=TILES)[:, u, :]
+            if u < SCALAR_PARTS:
+                nc.scalar.activation(z_bf[:, u, :, LAST], src, ACT.Copy, scale=ga_t[:, LAST : LAST + 1])
             else:
-                nc.vector.tensor_scalar(z_g[:, u, :, t], src, ga_t[:, t : t + 1], None, ALU.mult)
+                nc.vector.tensor_scalar(z_bf[:, u, :, LAST], src, ga_t[:, LAST : LAST + 1], None, ALU.mult)
 
         def s_tile(u):
-            z_c = sb(f"z_c{u}", [P, 128], U32)
-            z_s = sb(f"z_s{u}", [P, 128], U8)
-            nc.vector.quantize_mx(out=z_c[:].bitcast(FP8X4), scales=z_s[:], in_=z_g[:, u, :, :].rearrange("p m t -> p (m t)"))
-            parts = 2 if u == 0 else 1
-            width = V // parts
-            for h in range(parts):
-                cols = slice(h * width, (h + 1) * width)
-                bank = psum.tile([P, width], F32, name=f"s_bank{u}_{h}", tag=("bankb", "banka")[h] + str(u))
+            z_w = sbuf(f"z_w{u}", [P, P], U32)
+            z_s = sbuf(f"z_s{u}", [P, P], U8)
+            nc.vector.quantize_mx(out=z_w[:].bitcast(FP8X4), scales=z_s[:], in_=z_bf[:, u, :, :].rearrange("p m t -> p (m t)"))
+            parts = [("bank_b0", halves[0]), ("bank_a0", halves[1])] if u == 0 else [(f"bank_b{u}", whole)]
+            for tag, cols in parts:
+                bank = psum.tile([P, cols.stop - cols.start], F32, name=f"s_{tag}", tag=tag)
                 nc.tensor.matmul_mx(
                     out=bank[:],
-                    lhsT=z_c[:].bitcast(FP8X4),
+                    lhsT=z_w[:].bitcast(FP8X4),
                     lhsT_scale=z_s[:],
-                    rhs=z2_c[:, cols].bitcast(FP8X4),
+                    rhs=z2_w[:, cols].bitcast(FP8X4),
                     rhs_scale=z2_s[:, cols],
                     start=True,
                     stop=True,
                 )
-                nc.scalar.activation(s_t[u][:, cols], bank[:], ACT.Copy, scale=0.0625)
+                nc.scalar.activation(s[u][:, cols], bank[:], ACT.Copy, scale=0.0625)
 
-        z_last(0)
-        z_last(1)
+        z_round_last(0)
+        z_round_last(1)
         s_tile(0)
-        z_last(2)
+        z_round_last(2)
         s_tile(1)
-        z_last(3)
+        z_round_last(3)
         s_tile(2)
         s_tile(3)
 
-        pa2 = sb("pa2", [P, PACK, W], F32)
-        pb2 = sb("pb2", [P, PACK, W], F32)
-        rb2 = sb("rb2", [P, PACK, W], F32)
-        y = [sb(f"y{u}", [P, V], F32) for u in range(PACK)]
-        mag = sb("mag", [P, PACK * W], F32)
-        lg = sb("lg", [P, PACK * W], F32)
-        inv = sb("inv", [P, PACK, W], F32)
-        half = sb("half", [P, 1], F32)
-        nc.vector.memset(half[:], 0.5)
-        y_g = sb("y_g", [P, V, PACK], BF16)
-        out_rows = out_0.rearrange("(p u) v -> p u v", u=PACK)
+        pa2 = sbuf("pa2", [P, TILES, W], F32)
+        pb2 = sbuf("pb2", [P, TILES, W], F32)
+        rb2 = sbuf("rb2", [P, TILES, W], F32)
+        y = [sbuf(f"y{u}", [P, V], F32) for u in range(TILES)]
+        pb2_abs = sbuf("pb2_abs", [P, TILES * W], F32)
+        log_den = sbuf("log_den", [P, TILES * W], F32)
+        inv_den = sbuf("inv_den", [P, TILES, W], F32)
+        one_half = sbuf("one_half", [P, 1], F32)
+        nc.vector.memset(one_half[:], 0.5)
+        y_bf = sbuf("y_bf", [P, V, TILES], BF16)
+        out_rows = out_0.rearrange("(p u) v -> p u v", u=TILES)
 
-        for u in range(PACK):
-            nc.vector.tensor_copy(pb2[:, u, :], s_t[u][:].indirect(n6_l[:]))
-        nc.scalar.activation(mag[:], pb2[:].rearrange("p u w -> p (u w)"), ACT.Abs)
-        nc.scalar.activation(lg[:], mag[:], ACT.Ln, bias=half[:])
-        nc.scalar.activation(inv[:].rearrange("p u w -> p (u w)"), lg[:], ACT.Exp, scale=-1.0)
+        for u in range(TILES):
+            nc.vector.tensor_copy(pb2[:, u, :], s[u][:].indirect(n6_l[:]))
+        nc.scalar.activation(pb2_abs[:], pb2[:].rearrange("p u w -> p (u w)"), ACT.Abs)
+        nc.scalar.activation(log_den[:], pb2_abs[:], ACT.Ln, bias=one_half[:])
+        nc.scalar.activation(inv_den[:].rearrange("p u w -> p (u w)"), log_den[:], ACT.Exp, scale=-1.0)
 
-        def c_gather(u):
-            nc.vector.tensor_copy(pa2[:, u, :], s_t[u][:].indirect(n5_l[:]))
+        def s_gather(u):
+            nc.vector.tensor_copy(pa2[:, u, :], s[u][:].indirect(n5_l[:]))
 
-        def c_max(u):
+        def s_max_of_two_tiles(u):
             nc.vector.tensor_tensor(rb2[:, u : u + 2, :], pa2[:, u : u + 2, :], pb2[:, u : u + 2, :], ALU.max)
 
-        def c_put_max(u):
+        def s_put_max(u):
             nc.vector.tensor_copy(y[u][:].indirect(n6_l[:]), rb2[:, u, :])
 
-        def c_put_ratio(u):
-            nc.vector.tensor_tensor(y[u][:].indirect(n5_l[:]), pa2[:, u, :], inv[:, u, :], ALU.mult)
+        def s_put_ratio(u):
+            nc.vector.tensor_tensor(y[u][:].indirect(n5_l[:]), pa2[:, u, :], inv_den[:, u, :], ALU.mult)
             nc.sync.dma_start(out=out_rows[:, u, :], in_=y[u][:])
-            if u < PACK - 2:
-                nc.scalar.copy(y_g[:, :, u], y[u][:])
-            elif u == PACK - 2:
-                nc.scalar.copy(y_g[:, :, u : u + 2], y[u][:].unsqueeze(2).to_broadcast([P, V, 2]))
+            if u < LAST - 1:
+                nc.scalar.copy(y_bf[:, :, u], y[u][:])
+            elif u == LAST - 1:
+                nc.scalar.copy(y_bf[:, :, u : u + 2], y[u][:].unsqueeze(2).to_broadcast([P, V, 2]))
 
-        c_gather(0)
-        c_gather(1)
-        c_gather(2)
-        c_max(0)
-        c_gather(3)
-        c_put_max(0)
-        c_max(2)
-        c_put_max(1)
-        c_put_max(2)
-        c_put_max(3)
-        c_put_ratio(2)
-        c_put_ratio(0)
-        c_put_ratio(1)
-        c_put_ratio(3)
+        s_gather(0)
+        s_gather(1)
+        s_gather(2)
+        s_max_of_two_tiles(0)
+        s_gather(3)
+        s_put_max(0)
+        s_max_of_two_tiles(2)
+        for u in range(1, TILES):
+            s_put_max(u)
+        for u in (LAST - 1, 0, 1, LAST):
+            s_put_ratio(u)
 
-        y_c = sb("y_c", [P, V], U32)
-        y_s = sb("y_s", [P, V], U8)
-        words = out_1[0].rearrange("p n r -> p (n r)").bitcast(I32)
-        nc.vector.tensor_copy(y_g[:, 0:256, PACK - 1], y[PACK - 1][:, 0:256])
-        nc.vector.tensor_copy(y_g[:, 256:384, PACK - 1], y[PACK - 1][:, 256:384])
-        nc.scalar.copy(y_g[:, 384:512, PACK - 1], y[PACK - 1][:, 384:512])
-        for c0 in range(0, V, 256):
-            cols = slice(c0, c0 + 256)
-            nc.vector.quantize_mx(out=y_c[:, cols].bitcast(FP8X4), scales=y_s[:, cols], in_=y_g[:, cols, :].rearrange("p c t -> p (c t)"))
-            nc.sync.dma_start(out=words[:, cols], in_=y_c[:, cols].bitcast(I32))
-        rows = out_2[0].bitcast(I32)
-        for q in range(4):
-            eng = nc.scalar if q % 2 else nc.sync
-            eng.dma_start(out=rows[4 * q : 4 * q + 4, :], in_=y_s[:].bitcast(I32)[32 * q : 32 * q + 4, :])
+        y_w = sbuf("y_w", [P, V], U32)
+        y_s = sbuf("y_s", [P, V], U8)
+        out_words = out_1[0].rearrange("p n r -> p (n r)").bitcast(I32)
+        nc.vector.tensor_copy(y_bf[:, :HALF, LAST], y[LAST][:, :HALF])
+        nc.vector.tensor_copy(y_bf[:, HALF : V - QUARTER, LAST], y[LAST][:, HALF : V - QUARTER])
+        nc.scalar.copy(y_bf[:, V - QUARTER :, LAST], y[LAST][:, V - QUARTER :])
+        for cols in halves:
+            nc.vector.quantize_mx(out=y_w[:, cols].bitcast(FP8X4), scales=y_s[:, cols], in_=y_bf[:, cols, :].rearrange("p v u -> p (v u)"))
+            nc.sync.dma_start(out=out_words[:, cols], in_=y_w[:, cols].bitcast(I32))
+        out_scale_rows = out_2[0].bitcast(I32)
+        for q in range(QUADS):
+            queue = nc.scalar if q % 2 else nc.sync
+            queue.dma_start(out=out_scale_rows[4 * q : 4 * q + 4, :], in_=y_s[:].bitcast(I32)[32 * q : 32 * q + 4, :])

from contextlib import ExitStack

import concourse.mybir as mybir

T, S, V, H, W = 2048, 512, 512, 512, 256
FLOPS = 3 * 2 * 512 * 512 * 512

F32 = mybir.dt.float32
BF16 = mybir.dt.bfloat16
I32 = mybir.dt.int32
U32 = mybir.dt.uint32
U16 = mybir.dt.uint16
U8 = mybir.dt.uint8
FP8X4 = mybir.dt.float8_e4m3fn_x4
FP4X4 = mybir.dt.float4_e2m1fn_x4
ALU = mybir.AluOpType
ACT = mybir.ActivationFunctionType

P = 128
TILES = 4
LAST = TILES - 1
QUADS = 4
HALF = 256
QUARTER = 128
SCALAR_PARTS = 2


def tile_picked_kqbondsendgratio_none_po_kernel(
    tc, x_words, x_scales, w1_words, w1_scales, w2_words, w2_scales, ga, gb, offs, two, n1, n2, n3, n4, n5, n6, out_0, out_1, out_2
):
    nc = tc.nc
    with ExitStack() as ctx:
        keep = ctx.enter_context(tc.tile_pool(name="keep", bufs=1))
        psum = ctx.enter_context(tc.psum_pool(name="psum", bufs=1))

        def sbuf(name, shape, dtype, tag=None):
            return keep.tile(shape, dtype, name=name, tag=tag or name, align_bytes=64)

        def load_list(name, src):
            tile = keep.tile(list(src.shape), U16, name=name)
            nc.sync.dma_start(tile[:], src)
            return tile

        def load_scales(name, src, width, queues):
            tile = sbuf(name, [P, width], U8)
            nc.vector.memset(tile[:].bitcast(I32), 0)
            rows = src[0].bitcast(I32)
            for q in range(QUADS):
                queues[q % len(queues)].dma_start(out=tile[:].bitcast(I32)[32 * q : 32 * q + 4, :], in_=rows[4 * q : 4 * q + 4, :])
            return tile

        def load_fp4_words(name, words):
            tile = sbuf(name, [P, 2 * H], U8)
            nc.sync.dma_start(out=tile[:].bitcast(I32), in_=words[0].bitcast(I32))
            return tile

        def load_gain(name, src):
            gain = sbuf(name, [P, TILES], F32)
            view = src.rearrange("(q t i) o -> i q (t o)", t=TILES, i=4)
            with nc.allow_non_contiguous_dma(reason="one value for each feature"):
                for i in range(4):
                    nc.sync.dma_start(out=gain[i:P:4, :], in_=view[i])
            return gain

        def deal_weight(name, words, scales):
            dealt_words = sbuf(name + "_dealt_words", [P, 2 * H], U8)
            dealt_scales = sbuf(name + "_dealt_scales", [P, H], U8)
            nc.gpsimd.tensor_copy(
                out=dealt_words[:].bitcast(I32).rearrange("p (t q e) -> p t q e", t=TILES, e=2),
                in_=words[:].bitcast(I32).rearrange("p (q t e) -> p t q e", t=TILES, e=2),
            )
            nc.gpsimd.tensor_copy(
                out=dealt_scales[:].bitcast(I32).rearrange("p (t q) -> p t q", t=TILES),
                in_=scales[:].bitcast(I32).rearrange("p (q t) -> p t q", t=TILES),
            )
            return dealt_words, dealt_scales

        xs = load_scales("xs", x_scales, T, (nc.sync, nc.scalar))
        two_l = load_list("two_l", two)
        offs_l = load_list("offs_l", offs)
        w2_raw = load_fp4_words("w2_raw", w2_words)
        xw = sbuf("xw", [P, T], I32)
        nc.sync.dma_start(out=xw[:], in_=x_words[0].rearrange("p n r -> p (n r)").bitcast(I32))
        w2_raw_s = load_scales("w2_raw_s", w2_scales, H, (nc.sync,))
        n4_l = load_list("n4_l", n4)
        n3_l = load_list("n3_l", n3)
        w1_raw = load_fp4_words("w1_raw", w1_words)
        w1_raw_s = load_scales("w1_raw_s", w1_scales, H, (nc.sync,))
        n1_l = load_list("n1_l", n1)
        n2_l = load_list("n2_l", n2)
        gb_t = load_gain("gb_t", gb)
        ga_t = load_gain("ga_t", ga)
        n5_l = load_list("n5_l", n5)
        n6_l = load_list("n6_l", n6)

        xb_s = sbuf("xb_s", [P, V], U8)
        xa_s = sbuf("xa_s", [P, S], U8)
        xb_w = sbuf("xb_w", [P, V], U32)
        nc.vector.tensor_copy(xb_s[:], xs[:].indirect(two_l[:]))
        nc.vector.tensor_copy(xb_w[:], xw[:].bitcast(U32).indirect(two_l[:]))
        w2_w, w2_s = deal_weight("w2", w2_raw, w2_raw_s)
        nc.vector.tensor_copy(xa_s[:], xs[:].indirect(offs_l[:]))
        xa_w = sbuf("xa_w", [P, S], U32)
        nc.vector.tensor_copy(xa_w[:], xw[:].bitcast(U32).indirect(offs_l[:]))

        def project(tag, w_w, w_s, x_w, x_s, t, cols):
            bank = psum.tile([P, cols.stop - cols.start], F32, name=f"proj_{tag}_{t}", tag=tag)
            nc.tensor.matmul_mx(
                out=bank[:],
                lhsT=w_w[:, 2 * P * t : 2 * P * (t + 1)].bitcast(FP4X4),
                lhsT_scale=w_s[:, P * t : P * (t + 1)],
                rhs=x_w[:, cols].bitcast(FP8X4),
                rhs_scale=x_s[:, cols],
                start=True,
                stop=True,
            )
            return bank

        whole = slice(0, V)
        halves = (slice(0, HALF), slice(HALF, V))
        b_parts = [[("bank_b0", halves[0]), ("bank_a3", halves[1])]] + [[(f"bank_b{t}", whole)] for t in range(1, TILES)]
        b_banks = [[(project(tag, w2_w, w2_s, xb_w, xb_s, t, cols), cols) for tag, cols in b_parts[t]] for t in range(TILES)]

        b = [sbuf(f"b{t}", [P, 2 * V], F32) for t in range(TILES)]
        for t in range(TILES):
            for bank, cols in b_banks[t]:
                nc.scalar.copy(b[t][:, cols], bank[:])
        sig = [sbuf(f"sig{t}", [P, V], F32) for t in range(TILES)]
        for t in range(TILES):
            nc.scalar.activation(sig[t][:], b[t][:, :V], ACT.Sigmoid)

        b_n4 = [sbuf(f"b_n4_{t}", [P, V], F32) for t in range(TILES)]
        sm = [sbuf(f"sm{t}", [P, V], F32) for t in range(TILES)]
        ds2 = [sbuf(f"ds2_{t}", [P, 2 * V], F32) for t in range(TILES)]
        gated = [sbuf(f"gated{t}", [P, V], F32) for t in range(TILES)]
        z2_bf = sbuf("z2_bf", [P, V, TILES], BF16)

        def b_gather(t):
            nc.vector.tensor_copy(b_n4[t][:], b[t][:].indirect(n4_l[:]))

        def b_max(t):
            for bank, cols in b_banks[t]:
                nc.vector.tensor_tensor(sm[t][:, cols], b_n4[t][:, cols], bank[:], ALU.max)

        def b_scatter(t):
            nc.vector.tensor_copy(ds2[t][:].indirect(n3_l[:]), sm[t][:])

        def b_gate(t):
            nc.gpsimd.tensor_tensor(gated[t][:], ds2[t][:, :V], sig[t][:], ALU.mult)
            nc.scalar.activation(z2_bf[:, :, t], gated[t][:], ACT.Copy, scale=gb_t[:, t : t + 1])

        dt = [sbuf(f"dt{t}", [P, S], F32) for t in range(TILES)]

        b_gather(0)
        b_gather(1)
        b_max(0)
        b_gather(2)
        b_max(1)
        b_scatter(0)
        w1_w, w1_s = deal_weight("w1", w1_raw, w1_raw_s)
        a_banks = [project(f"bank_a{t}", w1_w, w1_s, xa_w, xa_s, t, whole) for t in range(TILES)]
        a = [sbuf(f"a{t}", [P, S], F32) for t in range(TILES)]
        for t in range(TILES):
            nc.scalar.copy(a[t][:], a_banks[t][:])
        b_gather(3)
        b_max(2)
        b_scatter(1)
        b_max(3)
        b_gate(0)
        b_scatter(2)
        b_gate(1)
        b_scatter(3)
        b_gate(2)
        b_gate(3)

        pab = {}

        def a_gather(t):
            if t % 2 == 0:
                pab[t // 2] = sbuf(f"pab{t // 2}", [P, 2, 2, W], F32, "sm2" if t == 0 else None)
            nc.vector.tensor_copy(pab[t // 2][:, t % 2, 0, :], a[t][:].indirect(n1_l[:]))
            nc.vector.tensor_copy(pab[t // 2][:, t % 2, 1, :], a[t][:].indirect(n2_l[:]))

        def a_put_sum(t):
            nc.vector.tensor_tensor(dt[t][:].indirect(n1_l[:]), pab[t // 2][:, t % 2, 0, :], pab[t // 2][:, t % 2, 1, :], ALU.add)

        def a_put_product(t):
            nc.vector.tensor_tensor(dt[t][:].indirect(n2_l[:]), pab[t // 2][:, t % 2, 0, :], pab[t // 2][:, t % 2, 1, :], ALU.mult)

        a_gather(0)

        z_bf = sbuf("z_bf", [P, TILES, P, TILES], BF16, "gated3")

        def z_round(t):
            src = dt[t][:].rearrange("p (m u) -> p m u", u=TILES)
            if t == LAST - 1:
                nc.scalar.activation(
                    z_bf[:, :, :, t : t + 2].rearrange("p u m e -> p m u e"),
                    src.unsqueeze(3).to_broadcast([P, P, TILES, 2]),
                    ACT.Copy,
                    scale=ga_t[:, t : t + 1],
                )
            else:
                nc.scalar.activation(z_bf[:, :, :, t].rearrange("p u m -> p m u"), src, ACT.Copy, scale=ga_t[:, t : t + 1])

        z2_w = sbuf("z2_w", [P, V], U32)
        z2_s = sbuf("z2_s", [P, V], U8)
        a_gather(1)
        a_put_sum(0)
        a_put_sum(1)
        a_put_product(0)
        z_round(0)
        a_gather(2)
        a_put_product(1)
        z_round(1)
        a_gather(3)
        a_put_sum(2)
        a_put_sum(3)
        a_put_product(2)
        z_round(2)
        a_put_product(3)
        nc.vector.quantize_mx(out=z2_w[:].bitcast(FP8X4), scales=z2_s[:], in_=z2_bf[:].rearrange("p v t -> p (v t)"))

        s = [sbuf(f"s{u}", [P, V], F32) for u in range(TILES)]

        def z_round_last(u):
            src = dt[LAST][:].rearrange("p (m u) -> p u m", u=TILES)[:, u, :]
            if u < SCALAR_PARTS:
                nc.scalar.activation(z_bf[:, u, :, LAST], src, ACT.Copy, scale=ga_t[:, LAST : LAST + 1])
            else:
                nc.vector.tensor_scalar(z_bf[:, u, :, LAST], src, ga_t[:, LAST : LAST + 1], None, ALU.mult)

        def s_tile(u):
            z_w = sbuf(f"z_w{u}", [P, P], U32)
            z_s = sbuf(f"z_s{u}", [P, P], U8)
            nc.vector.quantize_mx(out=z_w[:].bitcast(FP8X4), scales=z_s[:], in_=z_bf[:, u, :, :].rearrange("p m t -> p (m t)"))
            parts = [("bank_b0", halves[0]), ("bank_a0", halves[1])] if u == 0 else [(f"bank_b{u}", whole)]
            for tag, cols in parts:
                bank = psum.tile([P, cols.stop - cols.start], F32, name=f"s_{tag}", tag=tag)
                nc.tensor.matmul_mx(
                    out=bank[:],
                    lhsT=z_w[:].bitcast(FP8X4),
                    lhsT_scale=z_s[:],
                    rhs=z2_w[:, cols].bitcast(FP8X4),
                    rhs_scale=z2_s[:, cols],
                    start=True,
                    stop=True,
                )
                nc.scalar.activation(s[u][:, cols], bank[:], ACT.Copy, scale=0.0625)

        z_round_last(0)
        z_round_last(1)
        s_tile(0)
        z_round_last(2)
        s_tile(1)
        z_round_last(3)
        s_tile(2)
        s_tile(3)

        pa2 = sbuf("pa2", [P, TILES, W], F32)
        pb2 = sbuf("pb2", [P, TILES, W], F32)
        rb2 = sbuf("rb2", [P, TILES, W], F32)
        y = [sbuf(f"y{u}", [P, V], F32) for u in range(TILES)]
        pb2_abs = sbuf("pb2_abs", [P, TILES * W], F32)
        log_den = sbuf("log_den", [P, TILES * W], F32)
        inv_den = sbuf("inv_den", [P, TILES, W], F32)
        one_half = sbuf("one_half", [P, 1], F32)
        nc.vector.memset(one_half[:], 0.5)
        y_bf = sbuf("y_bf", [P, V, TILES], BF16)
        out_rows = out_0.rearrange("(p u) v -> p u v", u=TILES)

        for u in range(TILES):
            nc.vector.tensor_copy(pb2[:, u, :], s[u][:].indirect(n6_l[:]))
        nc.scalar.activation(pb2_abs[:], pb2[:].rearrange("p u w -> p (u w)"), ACT.Abs)
        nc.scalar.activation(log_den[:], pb2_abs[:], ACT.Ln, bias=one_half[:])
        nc.scalar.activation(inv_den[:].rearrange("p u w -> p (u w)"), log_den[:], ACT.Exp, scale=-1.0)

        def s_gather(u):
            nc.vector.tensor_copy(pa2[:, u, :], s[u][:].indirect(n5_l[:]))

        def s_max_of_two_tiles(u):
            nc.vector.tensor_tensor(rb2[:, u : u + 2, :], pa2[:, u : u + 2, :], pb2[:, u : u + 2, :], ALU.max)

        def s_put_max(u):
            nc.vector.tensor_copy(y[u][:].indirect(n6_l[:]), rb2[:, u, :])

        def s_put_ratio(u):
            nc.vector.tensor_tensor(y[u][:].indirect(n5_l[:]), pa2[:, u, :], inv_den[:, u, :], ALU.mult)
            nc.sync.dma_start(out=out_rows[:, u, :], in_=y[u][:])
            if u < LAST - 1:
                nc.scalar.copy(y_bf[:, :, u], y[u][:])
            elif u == LAST - 1:
                nc.scalar.copy(y_bf[:, :, u : u + 2], y[u][:].unsqueeze(2).to_broadcast([P, V, 2]))

        s_gather(0)
        s_gather(1)
        s_gather(2)
        s_max_of_two_tiles(0)
        s_gather(3)
        s_put_max(0)
        s_max_of_two_tiles(2)
        for u in range(1, TILES):
            s_put_max(u)
        for u in (LAST - 1, 0, 1, LAST):
            s_put_ratio(u)

        y_w = sbuf("y_w", [P, V], U32)
        y_s = sbuf("y_s", [P, V], U8)
        out_words = out_1[0].rearrange("p n r -> p (n r)").bitcast(I32)
        nc.vector.tensor_copy(y_bf[:, :HALF, LAST], y[LAST][:, :HALF])
        nc.vector.tensor_copy(y_bf[:, HALF : V - QUARTER, LAST], y[LAST][:, HALF : V - QUARTER])
        nc.scalar.copy(y_bf[:, V - QUARTER :, LAST], y[LAST][:, V - QUARTER :])
        for cols in halves:
            nc.vector.quantize_mx(out=y_w[:, cols].bitcast(FP8X4), scales=y_s[:, cols], in_=y_bf[:, cols, :].rearrange("p v u -> p (v u)"))
            nc.sync.dma_start(out=out_words[:, cols], in_=y_w[:, cols].bitcast(I32))
        out_scale_rows = out_2[0].bitcast(I32)
        for q in range(QUADS):
            queue = nc.scalar if q % 2 else nc.sync
            queue.dma_start(out=out_scale_rows[4 * q : 4 * q + 4, :], in_=y_s[:].bitcast(I32)[32 * q : 32 * q + 4, :])
